import numpy as np
import ml_dtypes


def mxq(x, axis, fmt="e4m3"):
    dtype, down = {"e4m3": (ml_dtypes.float8_e4m3fn, 7), "e5m2": (ml_dtypes.float8_e5m2, 14)}[fmt]
    v = np.moveaxis(np.asarray(x, np.float32).astype(ml_dtypes.bfloat16).astype(np.float64), axis, -1)
    blocks = v.reshape(v.shape[:-1] + (-1, 32))
    amax = np.abs(blocks).max(-1, keepdims=True)
    byte = np.maximum(np.where(amax > 0, np.frexp(amax)[1] - 1 + 127, 0) - down, 1)
    scale = np.exp2(byte - 127.0)
    codes = (blocks / scale).astype(np.float32).astype(dtype).astype(np.float64)
    return np.moveaxis((codes * scale).reshape(v.shape), -1, axis)


WIDE = False


def mx_kscale(k):
    if not WIDE:
        return np.ones(k)
    levels = np.array([10, -10, 5, -5, 0])
    if k % 512:
        return np.exp2(np.random.permutation(np.resize(levels, k // 32))).repeat(32)
    a = np.empty((k // 512, 16))
    for p in range(k // 512):
        a[p, :8] = np.random.permutation(np.resize(levels, 8))
        for g in range(8):
            far = levels[np.abs(levels - a[p, g]) >= 10]
            a[p, g + 8] = far[np.random.randint(len(far))]
    return np.exp2(a.ravel()).repeat(32)


def f64(x):
    return np.asarray(x).astype(np.float64)


def striped(idx):
    return np.tile(np.asarray(idx).reshape(-1, 16).T, (8, 1)).astype(np.uint16)


def unstriped(offs):
    return offs[:16].T.reshape(-1).astype(np.int64)


def striped8(idx):
    return np.asarray(idx).reshape(8, -1, 16).transpose(0, 2, 1).reshape(128, -1).astype(np.uint16)


def unstriped8(offs):
    return offs.reshape(8, 16, -1).transpose(0, 2, 1).reshape(8, -1).astype(np.int64)


def pick8(x, idx, run):
    r = np.arange(len(x))
    return x[r[:, None], idx[r % (8 * run) // run]]


E2M1 = np.array([0.0, 0.5, 1.0, 1.5, 2.0, 3.0, 4.0, 6.0, -0.0, -0.5, -1.0, -1.5, -2.0, -3.0, -4.0, -6.0])


def pack_weight(w, fmt):
    k, n = w.shape
    w = f64(np.asarray(w, np.float32).astype(ml_dtypes.bfloat16)).reshape(k // 32, 32, n)
    amax = np.abs(w).max(1)
    if fmt == "e4m3":
        byte = np.frexp(amax)[1] - 1 + 127 - 7
    else:
        mant, ex = np.frexp(amax / 6.0)
        byte = np.where(mant > 0.5, ex, ex - 1) + 127
    byte = np.clip(np.where(amax > 0, byte, 1), 1, 254)
    scaled = (w * np.exp2(127.0 - byte)[:, None, :]).reshape(k, n).astype(np.float32)
    by_word = np.ascontiguousarray(scaled.reshape(k // 512, 128, 4, n).transpose(0, 1, 3, 2))
    if fmt == "e4m3":
        words = by_word.astype(ml_dtypes.float8_e4m3fn).view(np.uint8)
    else:
        c = by_word.astype(ml_dtypes.float4_e2m1fn).view(np.uint8) & 0xF
        words = (c[..., 0::2] | (c[..., 1::2] << 4)).reshape(k // 512, 128, 2 * n)
    return np.ascontiguousarray(words), np.ascontiguousarray(byte.astype(np.uint8).reshape(k // 512, 16, n))


def unpack_weight(words, scales, fmt):
    g, _, n = scales.shape
    words = np.ascontiguousarray(words).reshape(g, 128, n, -1)
    if fmt == "e4m3":
        vals = words.view(ml_dtypes.float8_e4m3fn).astype(np.float64)
    else:
        nib = np.empty((g, 128, n, 4), np.uint8)
        nib[..., 0::2] = words & 0xF
        nib[..., 1::2] = words >> 4
        vals = E2M1[nib]
    vals = vals * np.repeat(np.exp2(scales.astype(np.float64) - 127.0), 8, axis=1)[..., None]
    return vals.transpose(0, 1, 3, 2).reshape(g * 512, n)


K, J, R, T, F, C, O, N, U = 512, 512, 512, 2048, 1024, 1024, 512, 256, 1024


def setup_inputs():
    n = np.random.standard_normal
    idx = np.random.permutation(T)[:J]
    idx2 = np.random.permutation(F)[:R]
    idx3 = np.stack([np.random.permutation(C)[:J] for _ in range(8)])
    idx4 = np.stack([np.random.permutation(C)[:J] for _ in range(8)])
    idx5 = np.stack([np.random.permutation(C)[:O] for _ in range(8)])
    idx6 = np.stack([np.random.permutation(C)[:O] for _ in range(8)])
    idx7 = np.stack([np.random.permutation(U)[:O] for _ in range(8)])
    fk = mx_kscale(K)
    fr = mx_kscale(R)
    tr = np.ones(F)
    tr[idx2] = fr
    xtp = pack_weight(n((K, T)) * fk[:, None], "e2m1")
    wtp = pack_weight(n((K, F)) * 1 / np.sqrt(K) / fk[:, None] * tr, "e4m3")
    wbp = pack_weight(n((R, N)) * 1 / np.sqrt(R) / fr[:, None], "e2m1")
    return {
        "xt_words": xtp[0],
        "xt_scales": xtp[1],
        "wt_words": wtp[0],
        "wt_scales": wtp[1],
        "sa": (np.random.uniform(0.5, 1.6, (R, 1))).astype(np.float32),
        "sb": (np.random.uniform(0.5, 1.6, (R, 1))).astype(np.float32),
        "wb_words": wbp[0],
        "wb_scales": wbp[1],
        "offs": striped(idx),
        "offs2": striped(idx2),
        "offs3": striped8(idx3),
        "offs4": striped8(idx4),
        "offs5": striped8(idx5),
        "offs6": striped8(idx6),
        "offs7": striped8(idx7),
    }


def reference(xt_words, xt_scales, wt_words, wt_scales, sa, sb, wb_words, wb_scales, offs, offs2, offs3, offs4, offs5, offs6, offs7):
    idx = unstriped(offs)
    idx2 = unstriped(offs2)
    idx3 = unstriped8(offs3)
    idx4 = unstriped8(offs4)
    idx5 = unstriped8(offs5)
    idx6 = unstriped8(offs6)
    idx7 = unstriped8(offs7)
    xtu = unpack_weight(xt_words, xt_scales, "e2m1")
    wtu = unpack_weight(wt_words, wt_scales, "e4m3")
    wbu = unpack_weight(wb_words, wb_scales, "e2m1")
    wtidx2g = wtu[:, idx2]
    xtidxg = xtu[:, idx]
    a = wtidx2g.T @ xtidxg
    g1 = np.pad(a, ((0, 0), (1, 0)))[:, :J]
    g2 = a - g1
    pw = np.zeros((R, C))
    pw[np.arange(R)[:, None], idx3[np.arange(R) % 512 // 64]] = a
    pv = np.zeros((R, C))
    pv[np.arange(R)[:, None], idx4[np.arange(R) % 512 // 64]] = g2
    hid = np.maximum(pick8(pw, idx5, 64) * f64(sa), pick8(pv, idx6, 64) * f64(sb))
    hidq = mxq(hid, 0, "e4m3")
    p = wbu.T @ hidq
    m0 = np.zeros((N, U))
    m0[np.arange(N)[:, None], idx7[np.arange(N) % 128 // 16]] = p
    m1 = np.pad(m0, ((0, 0), (1, 0)))[:, :U]
    y = m0 - m1
    return y

@@ -1,0 +1,216 @@
+from contextlib import ExitStack
+
+import concourse.mybir as mybir
+
+F32 = mybir.dt.float32
+BF16 = mybir.dt.bfloat16
+I32 = mybir.dt.int32
+U32 = mybir.dt.uint32
+U16 = mybir.dt.uint16
+U8 = mybir.dt.uint8
+FP8X4 = mybir.dt.float8_e4m3fn_x4
+FP4X4 = mybir.dt.float4_e2m1fn_x4
+COPY = mybir.ActivationFunctionType.Copy
+SUB = mybir.AluOpType.subtract
+MAX = mybir.AluOpType.max
+
+K, J, R, T, F, C, O, N, U = 512, 512, 512, 2048, 1024, 1024, 512, 256, 1024
+FLOPS = 2 * K * R * J + 2 * R * N * O
+P = 128
+PACK = 4
+HALF = 256
+LIST_COLS = 32
+HALF_COLS = 16
+LEAD = 8
+STORE_COLS = 256
+
+
+def tile_picked_tokens_store_one_changes_one_endsteps_kernel(
+    tc, xt_words, xt_scales, wt_words, wt_scales, sa, sb, wb_words, wb_scales,
+    offs, offs2, offs3, offs4, offs5, offs6, offs7, out,
+):
+    nc = tc.nc
+    with ExitStack() as ctx:
+        lists = ctx.enter_context(tc.tile_pool(name="lists", bufs=1))
+        pool = ctx.enter_context(tc.tile_pool(name="work", bufs=1))
+        psum = ctx.enter_context(tc.psum_pool(name="psum", bufs=1))
+
+        def sbuf(shape, dtype, name, tag=None):
+            return pool.tile(shape, dtype, name=name, tag=tag or name, align_bytes=64)
+
+        def load_list(source, name):
+            tile = lists.tile([P, LIST_COLS], U16, name=name, tag=name)
+            nc.sync.dma_start(tile[:], source)
+            return tile
+
+        def load_scales(tile, source, queue):
+            for q in range(4):
+                queue.dma_start(tile[32 * q : 32 * q + 4, :].bitcast(I32), source[0, 4 * q : 4 * q + 4, :].bitcast(I32))
+
+        def list_half(tile, h):
+            return tile[:, h * HALF_COLS : (h + 1) * HALF_COLS]
+
+        def half(h):
+            return slice(h * HALF, (h + 1) * HALF)
+
+        wt_s = sbuf([P, F], U8, "wt_s")
+        xt_s = sbuf([P, T], U8, "xt_s")
+        wb_s = sbuf([P, N], U8, "wb_s")
+        nc.gpsimd.memset(wt_s[:].bitcast(I32), 0)
+        nc.vector.memset(xt_s[:].bitcast(I32), 0)
+        nc.gpsimd.memset(wb_s[:].bitcast(I32), 0)
+        l2 = load_list(offs2, "l2")
+        l1 = load_list(offs, "l1")
+        load_scales(wt_s, wt_scales, nc.sync)
+        wt_w = sbuf([P, F], U32, "wt_w")
+        nc.sync.dma_start(wt_w[:].bitcast(I32), wt_words[0].rearrange("p n t -> p (n t)").bitcast(I32))
+        xt_w = sbuf([P, T], U16, "xt_w")
+        nc.sync.dma_start(xt_w[:].bitcast(I32), xt_words[0].bitcast(I32))
+        load_scales(xt_s, xt_scales, nc.sync)
+        l3 = load_list(offs3, "l3")
+        l4 = load_list(offs4, "l4")
+        l5 = load_list(offs5, "l5")
+        l6 = load_list(offs6, "l6")
+        sa_t = sbuf([P, PACK], F32, "sa_t")
+        sb_t = sbuf([P, PACK], F32, "sb_t")
+        nc.sync.dma_start(sa_t[:], sa.rearrange("(p t) o -> p (t o)", t=PACK))
+        nc.sync.dma_start(sb_t[:], sb.rearrange("(p t) o -> p (t o)", t=PACK))
+        l7 = load_list(offs7, "l7")
+        wb_w = sbuf([P, 2 * N], U8, "wb_w")
+        nc.sync.dma_start(wb_w[:].bitcast(I32), wb_words[0].bitcast(I32))
+        load_scales(wb_s, wb_scales, nc.sync)
+
+        board_w = [sbuf([P, C], F32, "board_w0")]
+        board_v = [sbuf([P, C], F32, "board_v0")]
+        nc.vector.memset(board_w[0][:], 0.0)
+        nc.vector.memset(board_v[0][:], 0.0)
+        a_sb = [sbuf([P, LEAD + J], F32, "a_sb%d" % t) for t in range(PACK)]
+        for t in range(PACK):
+            nc.gpsimd.memset(a_sb[t][:, LEAD - 1 : LEAD], 0.0)
+
+        w_s = sbuf([P, R], U8, "w_s")
+        w_w = sbuf([P, R], U32, "w_w")
+        nc.vector.tensor_copy(w_s[:].rearrange("p (t m) -> p m t", t=PACK), wt_s[:].indirect(l2[:]))
+        nc.vector.tensor_copy(w_w[:].rearrange("p (t m) -> p m t", t=PACK), wt_w[:].indirect(l2[:]))
+        x_s = sbuf([P, J], U8, "x_s")
+        x_w = sbuf([P, J], U16, "x_w")
+
+        def gather_tokens(h):
+            nc.vector.tensor_copy(x_w[:, half(h)], xt_w[:].indirect(list_half(l1, h)))
+            nc.vector.tensor_copy(x_s[:, half(h)], xt_s[:].indirect(list_half(l1, h)))
+
+        def first_product(t, cols, bank):
+            width = cols.stop - cols.start
+            acc = psum.tile([P, width], F32, name="acc_%s" % bank, tag=bank)
+            nc.tensor.matmul_mx(
+                out=acc[:],
+                lhsT=w_w[:, t * P : (t + 1) * P].bitcast(FP8X4),
+                lhsT_scale=w_s[:, t * P : (t + 1) * P],
+                rhs=x_w[:, cols].bitcast(FP4X4),
+                rhs_scale=x_s[:, cols],
+                start=True,
+                stop=True,
+            )
+            return acc
+
+        gather_tokens(0)
+        acc = first_product(0, half(0), "bank0")
+        nc.scalar.copy(a_sb[0][:, LEAD : LEAD + HALF], acc[:])
+        gather_tokens(1)
+        acc = first_product(0, half(1), "bank1")
+        nc.vector.tensor_copy(a_sb[0][:, LEAD + HALF : LEAD + J], acc[:])
+        change = [sbuf([P, J], F32, "change%d" % t) for t in range(PACK)]
+        for t in range(PACK):
+            if t > 0:
+                acc = first_product(t, slice(0, J), "bank%d" % (t + 1))
+                nc.vector.tensor_copy(a_sb[t][:, LEAD : LEAD + J], acc[:])
+            nc.vector.tensor_tensor(change[t][:], a_sb[t][:, LEAD : LEAD + J], a_sb[t][:, LEAD - 1 : LEAD + J - 1], SUB)
+
+        board_w.append(board_w[0])
+        board_v.append(board_v[0])
+        for t, (tag_w, tag_v) in ((2, ("w_w", "x_w")), (3, ("w_s", "x_s"))):
+            board_w.append(sbuf([P, C], F32, "board_w%d" % t, tag_w))
+            board_v.append(sbuf([P, C], F32, "board_v%d" % t, tag_v))
+            nc.vector.memset(board_w[t][:], 0.0)
+            nc.vector.memset(board_v[t][:], 0.0)
+
+        read_w = [[None, None] for t in range(PACK)]
+        read_v = [[None, None] for t in range(PACK)]
+        page = []
+        for t in range(PACK):
+            if t == 0:
+                for h in range(2):
+                    nc.scalar.activation(board_w[0][:].indirect(list_half(l3, h)), a_sb[0][:, LEAD + h * HALF : LEAD + (h + 1) * HALF], COPY)
+            else:
+                nc.scalar.activation(board_w[t][:].indirect(l3[:]), a_sb[t][:, LEAD : LEAD + J], COPY)
+            nc.scalar.activation(board_v[t][:].indirect(l4[:]), change[t][:], COPY)
+            if t == 0:
+                rw = sbuf([P, O], F32, "read_w0")
+                rv = sbuf([P, O], F32, "read_v0")
+                nc.scalar.activation(rw[:], board_w[0][:].indirect(l5[:]), COPY, scale=sa_t[:, 0:1])
+                nc.scalar.activation(rv[:], board_v[0][:].indirect(l6[:]), COPY, scale=sb_t[:, 0:1])
+                read_w[0] = [rw[:, half(0)], rw[:, half(1)]]
+                read_v[0] = [rv[:, half(0)], rv[:, half(1)]]
+                for nt, tag in enumerate(("a_sb0", "change0")):
+                    page.append(sbuf([P, U], F32, "page%d" % nt, tag))
+                    nc.vector.memset(page[nt][:], 0.0)
+            else:
+                rw = sbuf([P, HALF], F32, "read_w%d" % t)
+                rv = sbuf([P, HALF], F32, "read_v%d" % t)
+                nc.scalar.activation(rw[:], board_w[t][:].indirect(list_half(l5, 0)), COPY, scale=sa_t[:, t : t + 1])
+                nc.scalar.activation(rv[:], board_v[t][:].indirect(list_half(l6, 0)), COPY, scale=sb_t[:, t : t + 1])
+                read_w[t][0] = rw[:]
+                read_v[t][0] = rv[:]
+
+        def second_product(h, planes_tag, banks):
+            planes = sbuf([P, PACK, HALF], BF16, "planes%d" % h, planes_tag)
+            for t in range(PACK):
+                nc.vector.tensor_tensor(planes[:, t, :], read_w[t][h], read_v[t][h], MAX)
+            woven = sbuf([P, HALF, PACK], BF16, "woven%d" % h)
+            nc.vector.tensor_copy(
+                woven[:].rearrange("p (c i) t -> p c t i", i=4),
+                planes[:].rearrange("p t (c i) -> p c t i", i=4),
+            )
+            codes = sbuf([P, HALF], U32, "codes%d" % h)
+            scales = sbuf([P, HALF], U8, "scales%d" % h)
+            nc.vector.quantize_mx(codes[:].bitcast(FP8X4), scales[:], woven[:].rearrange("p o t -> p (o t)"))
+            results = []
+            for nt in range(2):
+                acc = psum.tile([P, HALF], F32, name="p_%d_%d" % (h, nt), tag=banks[nt])
+                nc.tensor.matmul_mx(
+                    out=acc[:],
+                    lhsT=wb_w[:, 2 * P * nt : 2 * P * (nt + 1)].bitcast(FP4X4),
+                    lhsT_scale=wb_s[:, P * nt : P * (nt + 1)],
+                    rhs=codes[:].bitcast(FP8X4),
+                    rhs_scale=scales[:],
+                    start=True,
+                    stop=True,
+                )
+                result = sbuf([P, HALF], F32, "result_%d_%d" % (h, nt))
+                nc.vector.tensor_copy(result[:], acc[:])
+                results.append(result)
+            return results
+
+        first = second_product(0, "planes0", ("bank5", "bank6"))
+
+        late = sbuf([P, 2 * (PACK - 1), HALF], F32, "late", "change3")
+        for t in range(1, PACK):
+            read_w[t][1] = late[:, 2 * t - 2, :]
+            read_v[t][1] = late[:, 2 * t - 1, :]
+            nc.scalar.activation(read_w[t][1], board_w[t][:].indirect(list_half(l5, 1)), COPY, scale=sa_t[:, t : t + 1])
+            nc.scalar.activation(read_v[t][1], board_v[t][:].indirect(list_half(l6, 1)), COPY, scale=sb_t[:, t : t + 1])
+        for nt in range(2):
+            nc.scalar.activation(page[nt][:].indirect(list_half(l7, 0)), first[nt][:], COPY)
+
+        second = second_product(1, "woven0", ("bank7", "bank0"))
+        for nt in range(2):
+            nc.scalar.activation(page[nt][:].indirect(list_half(l7, 1)), second[nt][:], COPY)
+            for piece in range(U // STORE_COLS):
+                lo, hi = piece * STORE_COLS, (piece + 1) * STORE_COLS
+                steps = sbuf([P, STORE_COLS], F32, "steps_%d_%d" % (nt, piece))
+                if piece == 0:
+                    nc.vector.tensor_copy(steps[:, 0:1], page[nt][:, 0:1])
+                    nc.vector.tensor_tensor(steps[:, 1:], page[nt][:, 1:hi], page[nt][:, 0 : hi - 1], SUB)
+                else:
+                    nc.vector.tensor_tensor(steps[:], page[nt][:, lo:hi], page[nt][:, lo - 1 : hi - 1], SUB)
+                nc.sync.dma_start(out[nt * P : (nt + 1) * P, lo:hi], steps[:])

@@ -60,14 +60,14 @@ def tile_picked_tokens_store_one_changes_one_endsteps_kernel(
         nc.vector.memset(xt_s[:].bitcast(I32), 0)
         nc.gpsimd.memset(wb_s[:].bitcast(I32), 0)
         l2 = load_list(offs2, "l2")
-        l1 = load_list(offs, "l1")
         load_scales(wt_s, wt_scales, nc.sync)
         wt_w = sbuf([P, F], U32, "wt_w")
         nc.sync.dma_start(wt_w[:].bitcast(I32), wt_words[0].rearrange("p n t -> p (n t)").bitcast(I32))
+        l1 = load_list(offs, "l1")
         xt_w = sbuf([P, T], U16, "xt_w")
         nc.sync.dma_start(xt_w[:].bitcast(I32), xt_words[0].bitcast(I32))
-        load_scales(xt_s, xt_scales, nc.sync)
         l3 = load_list(offs3, "l3")
+        load_scales(xt_s, xt_scales, nc.sync)
         l4 = load_list(offs4, "l4")
         l5 = load_list(offs5, "l5")
         l6 = load_list(offs6, "l6")
@@ -92,75 +92,78 @@ def tile_picked_tokens_store_one_changes_one_endsteps_kernel(
         w_w = sbuf([P, R], U32, "w_w")
         nc.vector.tensor_copy(w_s[:].rearrange("p (t m) -> p m t", t=PACK), wt_s[:].indirect(l2[:]))
         nc.vector.tensor_copy(w_w[:].rearrange("p (t m) -> p m t", t=PACK), wt_w[:].indirect(l2[:]))
-        x_s = sbuf([P, J], U8, "x_s")
-        x_w = sbuf([P, J], U16, "x_w")
-
-        def gather_tokens(h):
-            nc.vector.tensor_copy(x_w[:, half(h)], xt_w[:].indirect(list_half(l1, h)))
-            nc.vector.tensor_copy(x_s[:, half(h)], xt_s[:].indirect(list_half(l1, h)))
-
-        def first_product(t, cols, bank):
-            width = cols.stop - cols.start
-            acc = psum.tile([P, width], F32, name="acc_%s" % bank, tag=bank)
-            nc.tensor.matmul_mx(
-                out=acc[:],
-                lhsT=w_w[:, t * P : (t + 1) * P].bitcast(FP8X4),
-                lhsT_scale=w_s[:, t * P : (t + 1) * P],
-                rhs=x_w[:, cols].bitcast(FP4X4),
-                rhs_scale=x_s[:, cols],
-                start=True,
-                stop=True,
-            )
-            return acc
-
-        gather_tokens(0)
-        acc = first_product(0, half(0), "bank0")
-        nc.scalar.copy(a_sb[0][:, LEAD : LEAD + HALF], acc[:])
-        gather_tokens(1)
-        acc = first_product(0, half(1), "bank1")
-        nc.vector.tensor_copy(a_sb[0][:, LEAD + HALF : LEAD + J], acc[:])
         change = [sbuf([P, J], F32, "change%d" % t) for t in range(PACK)]
-        for t in range(PACK):
-            if t > 0:
-                acc = first_product(t, slice(0, J), "bank%d" % (t + 1))
-                nc.vector.tensor_copy(a_sb[t][:, LEAD : LEAD + J], acc[:])
-            nc.vector.tensor_tensor(change[t][:], a_sb[t][:, LEAD : LEAD + J], a_sb[t][:, LEAD - 1 : LEAD + J - 1], SUB)
+        whole = [psum.tile([P, J], F32, name="acc%d" % t, tag="bank%d" % (t + 1)) for t in range(1, PACK)]
+
+        def first_products(h):
+            x_w = sbuf([P, HALF], U16, "x_w%d" % h, "x_w")
+            x_s = sbuf([P, HALF], U8, "x_s%d" % h, "x_s")
+            nc.vector.tensor_copy(x_w[:], xt_w[:].indirect(list_half(l1, h)))
+            nc.vector.tensor_copy(x_s[:], xt_s[:].indirect(list_half(l1, h)))
+            lead = psum.tile([P, HALF], F32, name="acc0_%d" % h, tag="bank%d" % h)
+            for t in range(PACK):
+                nc.tensor.matmul_mx(
+                    out=lead[:] if t == 0 else whole[t - 1][:, half(h)],
+                    lhsT=w_w[:, t * P : (t + 1) * P].bitcast(FP8X4),
+                    lhsT_scale=w_s[:, t * P : (t + 1) * P],
+                    rhs=x_w[:].bitcast(FP4X4),
+                    rhs_scale=x_s[:],
+                    start=True,
+                    stop=True,
+                )
+            return lead
+
+        for h in range(2):
+            lo, hi = LEAD + h * HALF, LEAD + (h + 1) * HALF
+            lead = first_products(h)
+            nc.vector.tensor_copy(a_sb[0][:, lo:hi], lead[:])
+            nc.vector.tensor_tensor(change[0][:, half(h)], a_sb[0][:, lo:hi], a_sb[0][:, lo - 1 : hi - 1], SUB)
+        def cleared(name, tag):
+            tile = sbuf([P, C], F32, name, tag)
+            nc.vector.memset(tile[:], 0.0)
+            return tile
 
         board_w.append(board_w[0])
         board_v.append(board_v[0])
-        for t, (tag_w, tag_v) in ((2, ("w_w", "x_w")), (3, ("w_s", "x_s"))):
-            board_w.append(sbuf([P, C], F32, "board_w%d" % t, tag_w))
-            board_v.append(sbuf([P, C], F32, "board_v%d" % t, tag_v))
-            nc.vector.memset(board_w[t][:], 0.0)
-            nc.vector.memset(board_v[t][:], 0.0)
+        early_tags = {2: ("w_w", "w_s"), 3: ("x_w", "x_s")}
+        for t in range(1, PACK):
+            nc.vector.tensor_copy(a_sb[t][:, LEAD : LEAD + J], whole[t - 1][:])
+            if t in early_tags:
+                board_w.append(cleared("board_w%d" % t, early_tags[t][0]))
+            nc.vector.tensor_tensor(change[t][:], a_sb[t][:, LEAD : LEAD + J], a_sb[t][:, LEAD - 1 : LEAD + J - 1], SUB)
+            if t in early_tags:
+                board_v.append(cleared("board_v%d" % t, early_tags[t][1]))
 
         read_w = [[None, None] for t in range(PACK)]
         read_v = [[None, None] for t in range(PACK)]
+
+        def read_boards(t, h):
+            nc.scalar.activation(read_w[t][h], board_w[t][:].indirect(list_half(l5, h)), COPY, scale=sa_t[:, t : t + 1])
+            nc.scalar.activation(read_v[t][h], board_v[t][:].indirect(list_half(l6, h)), COPY, scale=sb_t[:, t : t + 1])
+
         page = []
+        early = sbuf([P, 2 * (PACK - 1), HALF], F32, "early")
         for t in range(PACK):
             if t == 0:
                 for h in range(2):
                     nc.scalar.activation(board_w[0][:].indirect(list_half(l3, h)), a_sb[0][:, LEAD + h * HALF : LEAD + (h + 1) * HALF], COPY)
+                    nc.scalar.activation(board_v[0][:].indirect(list_half(l4, h)), change[0][:, half(h)], COPY)
+                page.append(cleared("page0", "a_sb0"))
+                page.append(cleared("page1", "change0"))
             else:
                 nc.scalar.activation(board_w[t][:].indirect(l3[:]), a_sb[t][:, LEAD : LEAD + J], COPY)
-            nc.scalar.activation(board_v[t][:].indirect(l4[:]), change[t][:], COPY)
+                nc.scalar.activation(board_v[t][:].indirect(l4[:]), change[t][:], COPY)
             if t == 0:
-                rw = sbuf([P, O], F32, "read_w0")
-                rv = sbuf([P, O], F32, "read_v0")
-                nc.scalar.activation(rw[:], board_w[0][:].indirect(l5[:]), COPY, scale=sa_t[:, 0:1])
-                nc.scalar.activation(rv[:], board_v[0][:].indirect(l6[:]), COPY, scale=sb_t[:, 0:1])
-                read_w[0] = [rw[:, half(0)], rw[:, half(1)]]
-                read_v[0] = [rv[:, half(0)], rv[:, half(1)]]
-                for nt, tag in enumerate(("a_sb0", "change0")):
-                    page.append(sbuf([P, U], F32, "page%d" % nt, tag))
-                    nc.vector.memset(page[nt][:], 0.0)
+                both_w = sbuf([P, O], F32, "both_w")
+                both_v = sbuf([P, O], F32, "both_v")
+                nc.scalar.activation(both_w[:], board_w[0][:].indirect(l5[:]), COPY, scale=sa_t[:, 0:1])
+                nc.scalar.activation(both_v[:], board_v[0][:].indirect(l6[:]), COPY, scale=sb_t[:, 0:1])
+                read_w[0] = [both_w[:, half(0)], both_w[:, half(1)]]
+                read_v[0] = [both_v[:, half(0)], both_v[:, half(1)]]
             else:
-                rw = sbuf([P, HALF], F32, "read_w%d" % t)
-                rv = sbuf([P, HALF], F32, "read_v%d" % t)
-                nc.scalar.activation(rw[:], board_w[t][:].indirect(list_half(l5, 0)), COPY, scale=sa_t[:, t : t + 1])
-                nc.scalar.activation(rv[:], board_v[t][:].indirect(list_half(l6, 0)), COPY, scale=sb_t[:, t : t + 1])
-                read_w[t][0] = rw[:]
-                read_v[t][0] = rv[:]
+                read_w[t][0] = early[:, 2 * t - 2, :]
+                read_v[t][0] = early[:, 2 * t - 1, :]
+                read_boards(t, 0)
 
         def second_product(h, planes_tag, banks):
             planes = sbuf([P, PACK, HALF], BF16, "planes%d" % h, planes_tag)
@@ -197,8 +200,7 @@ def tile_picked_tokens_store_one_changes_one_endsteps_kernel(
         for t in range(1, PACK):
             read_w[t][1] = late[:, 2 * t - 2, :]
             read_v[t][1] = late[:, 2 * t - 1, :]
-            nc.scalar.activation(read_w[t][1], board_w[t][:].indirect(list_half(l5, 1)), COPY, scale=sa_t[:, t : t + 1])
-            nc.scalar.activation(read_v[t][1], board_v[t][:].indirect(list_half(l6, 1)), COPY, scale=sb_t[:, t : t + 1])
+            read_boards(t, 1)
         for nt in range(2):
             nc.scalar.activation(page[nt][:].indirect(list_half(l7, 0)), first[nt][:], COPY)
 
@@ -209,7 +211,10 @@ def tile_picked_tokens_store_one_changes_one_endsteps_kernel(
                 lo, hi = piece * STORE_COLS, (piece + 1) * STORE_COLS
                 steps = sbuf([P, STORE_COLS], F32, "steps_%d_%d" % (nt, piece))
                 if piece == 0:
-                    nc.vector.tensor_copy(steps[:, 0:1], page[nt][:, 0:1])
+                    if nt == 0:
+                        nc.vector.tensor_copy(steps[:, 0:1], page[nt][:, 0:1])
+                    else:
+                        nc.scalar.copy(steps[:, 0:1], page[nt][:, 0:1])
                     nc.vector.tensor_tensor(steps[:, 1:], page[nt][:, 1:hi], page[nt][:, 0 : hi - 1], SUB)
                 else:
                     nc.vector.tensor_tensor(steps[:], page[nt][:, lo:hi], page[nt][:, lo - 1 : hi - 1], SUB)

@@ -43,9 +43,9 @@ def tile_picked_tokens_store_one_changes_one_endsteps_kernel(
             nc.sync.dma_start(tile[:], source)
             return tile
 
-        def load_scales(tile, source, queue):
+        def load_scales(tile, source, queues):
             for q in range(4):
-                queue.dma_start(tile[32 * q : 32 * q + 4, :].bitcast(I32), source[0, 4 * q : 4 * q + 4, :].bitcast(I32))
+                queues[q % len(queues)].dma_start(tile[32 * q : 32 * q + 4, :].bitcast(I32), source[0, 4 * q : 4 * q + 4, :].bitcast(I32))
 
         def list_half(tile, h):
             return tile[:, h * HALF_COLS : (h + 1) * HALF_COLS]
@@ -60,14 +60,14 @@ def tile_picked_tokens_store_one_changes_one_endsteps_kernel(
         nc.vector.memset(xt_s[:].bitcast(I32), 0)
         nc.gpsimd.memset(wb_s[:].bitcast(I32), 0)
         l2 = load_list(offs2, "l2")
-        load_scales(wt_s, wt_scales, nc.sync)
+        load_scales(wt_s, wt_scales, (nc.sync,))
         wt_w = sbuf([P, F], U32, "wt_w")
         nc.sync.dma_start(wt_w[:].bitcast(I32), wt_words[0].rearrange("p n t -> p (n t)").bitcast(I32))
         l1 = load_list(offs, "l1")
+        l3 = load_list(offs3, "l3")
+        load_scales(xt_s, xt_scales, (nc.sync,))
         xt_w = sbuf([P, T], U16, "xt_w")
         nc.sync.dma_start(xt_w[:].bitcast(I32), xt_words[0].bitcast(I32))
-        l3 = load_list(offs3, "l3")
-        load_scales(xt_s, xt_scales, nc.sync)
         l4 = load_list(offs4, "l4")
         l5 = load_list(offs5, "l5")
         l6 = load_list(offs6, "l6")
@@ -78,7 +78,7 @@ def tile_picked_tokens_store_one_changes_one_endsteps_kernel(
         l7 = load_list(offs7, "l7")
         wb_w = sbuf([P, 2 * N], U8, "wb_w")
         nc.sync.dma_start(wb_w[:].bitcast(I32), wb_words[0].bitcast(I32))
-        load_scales(wb_s, wb_scales, nc.sync)
+        load_scales(wb_s, wb_scales, (nc.sync,))
 
         board_w = [sbuf([P, C], F32, "board_w0")]
         board_v = [sbuf([P, C], F32, "board_v0")]
@@ -95,29 +95,34 @@ def tile_picked_tokens_store_one_changes_one_endsteps_kernel(
         change = [sbuf([P, J], F32, "change%d" % t) for t in range(PACK)]
         whole = [psum.tile([P, J], F32, name="acc%d" % t, tag="bank%d" % (t + 1)) for t in range(1, PACK)]
 
-        def first_products(h):
-            x_w = sbuf([P, HALF], U16, "x_w%d" % h, "x_w")
-            x_s = sbuf([P, HALF], U8, "x_s%d" % h, "x_s")
-            nc.vector.tensor_copy(x_w[:], xt_w[:].indirect(list_half(l1, h)))
-            nc.vector.tensor_copy(x_s[:], xt_s[:].indirect(list_half(l1, h)))
-            lead = psum.tile([P, HALF], F32, name="acc0_%d" % h, tag="bank%d" % h)
-            for t in range(PACK):
-                nc.tensor.matmul_mx(
-                    out=lead[:] if t == 0 else whole[t - 1][:, half(h)],
-                    lhsT=w_w[:, t * P : (t + 1) * P].bitcast(FP8X4),
-                    lhsT_scale=w_s[:, t * P : (t + 1) * P],
-                    rhs=x_w[:].bitcast(FP4X4),
-                    rhs_scale=x_s[:],
-                    start=True,
-                    stop=True,
-                )
-            return lead
+        lead_pieces = (((0, 256, "bank0"),), ((256, 512, "bank1"),))
+
+        def first_product(t, acc, x_w, x_s):
+            nc.tensor.matmul_mx(
+                out=acc,
+                lhsT=w_w[:, t * P : (t + 1) * P].bitcast(FP8X4),
+                lhsT_scale=w_s[:, t * P : (t + 1) * P],
+                rhs=x_w.bitcast(FP4X4),
+                rhs_scale=x_s,
+                start=True,
+                stop=True,
+            )
 
         for h in range(2):
+            x_w = sbuf([P, HALF], U16, "x_w%d" % h, "x_w")
+            x_s = sbuf([P, HALF], U8, "x_s%d" % h, "x_s")
+            nc.vector.tensor_copy(x_s[:], xt_s[:].indirect(list_half(l1, h)))
+            nc.vector.tensor_copy(x_w[:], xt_w[:].indirect(list_half(l1, h)))
+            for lo, hi, bank in lead_pieces[h]:
+                lead = psum.tile([P, hi - lo], F32, name="lead%d" % lo, tag=bank)
+                cols = slice(lo - h * HALF, hi - h * HALF)
+                first_product(0, lead[:], x_w[:, cols], x_s[:, cols])
+                nc.vector.tensor_copy(a_sb[0][:, LEAD + lo : LEAD + hi], lead[:])
+            for t in range(1, PACK):
+                first_product(t, whole[t - 1][:, half(h)], x_w[:], x_s[:])
             lo, hi = LEAD + h * HALF, LEAD + (h + 1) * HALF
-            lead = first_products(h)
-            nc.vector.tensor_copy(a_sb[0][:, lo:hi], lead[:])
             nc.vector.tensor_tensor(change[0][:, half(h)], a_sb[0][:, lo:hi], a_sb[0][:, lo - 1 : hi - 1], SUB)
+
         def cleared(name, tag):
             tile = sbuf([P, C], F32, name, tag)
             nc.vector.memset(tile[:], 0.0)
@@ -146,7 +151,8 @@ def tile_picked_tokens_store_one_changes_one_endsteps_kernel(
         for t in range(PACK):
             if t == 0:
                 for h in range(2):
-                    nc.scalar.activation(board_w[0][:].indirect(list_half(l3, h)), a_sb[0][:, LEAD + h * HALF : LEAD + (h + 1) * HALF], COPY)
+                    for lo, hi, bank in lead_pieces[h]:
+                        nc.scalar.activation(board_w[0][:].indirect(l3[:, lo // 16 : hi // 16]), a_sb[0][:, LEAD + lo : LEAD + hi], COPY)
                     nc.scalar.activation(board_v[0][:].indirect(list_half(l4, h)), change[0][:, half(h)], COPY)
                 page.append(cleared("page0", "a_sb0"))
                 page.append(cleared("page1", "change0"))
@@ -167,16 +173,21 @@ def tile_picked_tokens_store_one_changes_one_endsteps_kernel(
 
         def second_product(h, planes_tag, banks):
             planes = sbuf([P, PACK, HALF], BF16, "planes%d" % h, planes_tag)
-            for t in range(PACK):
+            for t in range(PACK - 1):
                 nc.vector.tensor_tensor(planes[:, t, :], read_w[t][h], read_v[t][h], MAX)
+            quarters = (slice(0, HALF // 2), slice(HALF // 2, HALF))
+            for cols in quarters:
+                nc.vector.tensor_tensor(planes[:, PACK - 1, cols], read_w[PACK - 1][h][:, cols], read_v[PACK - 1][h][:, cols], MAX)
             woven = sbuf([P, HALF, PACK], BF16, "woven%d" % h)
-            nc.vector.tensor_copy(
-                woven[:].rearrange("p (c i) t -> p c t i", i=4),
-                planes[:].rearrange("p t (c i) -> p c t i", i=4),
-            )
+            for cols in quarters:
+                nc.vector.tensor_copy(
+                    woven[:, cols, :].rearrange("p (c i) t -> p c t i", i=4),
+                    planes[:, :, cols].rearrange("p t (c i) -> p c t i", i=4),
+                )
             codes = sbuf([P, HALF], U32, "codes%d" % h)
             scales = sbuf([P, HALF], U8, "scales%d" % h)
-            nc.vector.quantize_mx(codes[:].bitcast(FP8X4), scales[:], woven[:].rearrange("p o t -> p (o t)"))
+            for cols in quarters:
+                nc.vector.quantize_mx(codes[:, cols].bitcast(FP8X4), scales[:, cols], woven[:, cols, :].rearrange("p o t -> p (o t)"))
             results = []
             for nt in range(2):
                 acc = psum.tile([P, HALF], F32, name="p_%d_%d" % (h, nt), tag=banks[nt])

from contextlib import ExitStack

import concourse.mybir as mybir

F32 = mybir.dt.float32
BF16 = mybir.dt.bfloat16
I32 = mybir.dt.int32
U32 = mybir.dt.uint32
U16 = mybir.dt.uint16
U8 = mybir.dt.uint8
FP8X4 = mybir.dt.float8_e4m3fn_x4
FP4X4 = mybir.dt.float4_e2m1fn_x4
COPY = mybir.ActivationFunctionType.Copy
SUB = mybir.AluOpType.subtract
MAX = mybir.AluOpType.max

K, J, R, T, F, C, O, N, U = 512, 512, 512, 2048, 1024, 1024, 512, 256, 1024
FLOPS = 2 * K * R * J + 2 * R * N * O
P = 128
PACK = 4
HALF = 256
LIST_COLS = 32
HALF_COLS = 16
LEAD = 8
STORE_COLS = 256


def tile_picked_tokens_store_one_changes_one_endsteps_kernel(
    tc, xt_words, xt_scales, wt_words, wt_scales, sa, sb, wb_words, wb_scales,
    offs, offs2, offs3, offs4, offs5, offs6, offs7, out,
):
    nc = tc.nc
    with ExitStack() as ctx:
        lists = ctx.enter_context(tc.tile_pool(name="lists", bufs=1))
        pool = ctx.enter_context(tc.tile_pool(name="work", bufs=1))
        psum = ctx.enter_context(tc.psum_pool(name="psum", bufs=1))

        def sbuf(shape, dtype, name, tag=None):
            return pool.tile(shape, dtype, name=name, tag=tag or name, align_bytes=64)

        def load_list(source, name):
            tile = lists.tile([P, LIST_COLS], U16, name=name, tag=name)
            nc.sync.dma_start(tile[:], source)
            return tile

        def load_scales(tile, source, queues):
            for q in range(4):
                queues[q % len(queues)].dma_start(tile[32 * q : 32 * q + 4, :].bitcast(I32), source[0, 4 * q : 4 * q + 4, :].bitcast(I32))

        def list_half(tile, h):
            return tile[:, h * HALF_COLS : (h + 1) * HALF_COLS]

        def half(h):
            return slice(h * HALF, (h + 1) * HALF)

        wt_s = sbuf([P, F], U8, "wt_s")
        xt_s = sbuf([P, T], U8, "xt_s")
        wb_s = sbuf([P, N], U8, "wb_s")
        nc.gpsimd.memset(wt_s[:].bitcast(I32), 0)
        nc.vector.memset(xt_s[:].bitcast(I32), 0)
        nc.gpsimd.memset(wb_s[:].bitcast(I32), 0)
        l2 = load_list(offs2, "l2")
        load_scales(wt_s, wt_scales, (nc.sync,))
        wt_w = sbuf([P, F], U32, "wt_w")
        nc.sync.dma_start(wt_w[:].bitcast(I32), wt_words[0].rearrange("p n t -> p (n t)").bitcast(I32))
        l1 = load_list(offs, "l1")
        l3 = load_list(offs3, "l3")
        load_scales(xt_s, xt_scales, (nc.sync,))
        xt_w = sbuf([P, T], U16, "xt_w")
        nc.sync.dma_start(xt_w[:].bitcast(I32), xt_words[0].bitcast(I32))
        l4 = load_list(offs4, "l4")
        l5 = load_list(offs5, "l5")
        l6 = load_list(offs6, "l6")
        sa_t = sbuf([P, PACK], F32, "sa_t")
        sb_t = sbuf([P, PACK], F32, "sb_t")
        nc.sync.dma_start(sa_t[:], sa.rearrange("(p t) o -> p (t o)", t=PACK))
        nc.sync.dma_start(sb_t[:], sb.rearrange("(p t) o -> p (t o)", t=PACK))
        l7 = load_list(offs7, "l7")
        wb_w = sbuf([P, 2 * N], U8, "wb_w")
        nc.sync.dma_start(wb_w[:].bitcast(I32), wb_words[0].bitcast(I32))
        load_scales(wb_s, wb_scales, (nc.sync,))

        board_w = [sbuf([P, C], F32, "board_w0")]
        board_v = [sbuf([P, C], F32, "board_v0")]
        nc.vector.memset(board_w[0][:], 0.0)
        nc.vector.memset(board_v[0][:], 0.0)
        a_sb = [sbuf([P, LEAD + J], F32, "a_sb%d" % t) for t in range(PACK)]
        for t in range(PACK):
            nc.gpsimd.memset(a_sb[t][:, LEAD - 1 : LEAD], 0.0)

        w_s = sbuf([P, R], U8, "w_s")
        w_w = sbuf([P, R], U32, "w_w")
        nc.vector.tensor_copy(w_s[:].rearrange("p (t m) -> p m t", t=PACK), wt_s[:].indirect(l2[:]))
        nc.vector.tensor_copy(w_w[:].rearrange("p (t m) -> p m t", t=PACK), wt_w[:].indirect(l2[:]))
        change = [sbuf([P, J], F32, "change%d" % t) for t in range(PACK)]
        whole = [psum.tile([P, J], F32, name="acc%d" % t, tag="bank%d" % (t + 1)) for t in range(1, PACK)]

        lead_pieces = (((0, 256, "bank0"),), ((256, 512, "bank1"),))

        def first_product(t, acc, x_w, x_s):
            nc.tensor.matmul_mx(
                out=acc,
                lhsT=w_w[:, t * P : (t + 1) * P].bitcast(FP8X4),
                lhsT_scale=w_s[:, t * P : (t + 1) * P],
                rhs=x_w.bitcast(FP4X4),
                rhs_scale=x_s,
                start=True,
                stop=True,
            )

        for h in range(2):
            x_w = sbuf([P, HALF], U16, "x_w%d" % h, "x_w")
            x_s = sbuf([P, HALF], U8, "x_s%d" % h, "x_s")
            nc.vector.tensor_copy(x_s[:], xt_s[:].indirect(list_half(l1, h)))
            nc.vector.tensor_copy(x_w[:], xt_w[:].indirect(list_half(l1, h)))
            for lo, hi, bank in lead_pieces[h]:
                lead = psum.tile([P, hi - lo], F32, name="lead%d" % lo, tag=bank)
                cols = slice(lo - h * HALF, hi - h * HALF)
                first_product(0, lead[:], x_w[:, cols], x_s[:, cols])
                nc.vector.tensor_copy(a_sb[0][:, LEAD + lo : LEAD + hi], lead[:])
            for t in range(1, PACK):
                first_product(t, whole[t - 1][:, half(h)], x_w[:], x_s[:])
            lo, hi = LEAD + h * HALF, LEAD + (h + 1) * HALF
            nc.vector.tensor_tensor(change[0][:, half(h)], a_sb[0][:, lo:hi], a_sb[0][:, lo - 1 : hi - 1], SUB)

        def cleared(name, tag):
            tile = sbuf([P, C], F32, name, tag)
            nc.vector.memset(tile[:], 0.0)
            return tile

        board_w.append(board_w[0])
        board_v.append(board_v[0])
        early_tags = {2: ("w_w", "w_s"), 3: ("x_w", "x_s")}
        for t in range(1, PACK):
            nc.vector.tensor_copy(a_sb[t][:, LEAD : LEAD + J], whole[t - 1][:])
            if t in early_tags:
                board_w.append(cleared("board_w%d" % t, early_tags[t][0]))
            nc.vector.tensor_tensor(change[t][:], a_sb[t][:, LEAD : LEAD + J], a_sb[t][:, LEAD - 1 : LEAD + J - 1], SUB)
            if t in early_tags:
                board_v.append(cleared("board_v%d" % t, early_tags[t][1]))

        read_w = [[None, None] for t in range(PACK)]
        read_v = [[None, None] for t in range(PACK)]

        def read_boards(t, h):
            nc.scalar.activation(read_w[t][h], board_w[t][:].indirect(list_half(l5, h)), COPY, scale=sa_t[:, t : t + 1])
            nc.scalar.activation(read_v[t][h], board_v[t][:].indirect(list_half(l6, h)), COPY, scale=sb_t[:, t : t + 1])

        page = []
        early = sbuf([P, 2 * (PACK - 1), HALF], F32, "early")
        for t in range(PACK):
            if t == 0:
                for h in range(2):
                    for lo, hi, bank in lead_pieces[h]:
                        nc.scalar.activation(board_w[0][:].indirect(l3[:, lo // 16 : hi // 16]), a_sb[0][:, LEAD + lo : LEAD + hi], COPY)
                    nc.scalar.activation(board_v[0][:].indirect(list_half(l4, h)), change[0][:, half(h)], COPY)
                page.append(cleared("page0", "a_sb0"))
                page.append(cleared("page1", "change0"))
            else:
                nc.scalar.activation(board_w[t][:].indirect(l3[:]), a_sb[t][:, LEAD : LEAD + J], COPY)
                nc.scalar.activation(board_v[t][:].indirect(l4[:]), change[t][:], COPY)
            if t == 0:
                both_w = sbuf([P, O], F32, "both_w")
                both_v = sbuf([P, O], F32, "both_v")
                nc.scalar.activation(both_w[:], board_w[0][:].indirect(l5[:]), COPY, scale=sa_t[:, 0:1])
                nc.scalar.activation(both_v[:], board_v[0][:].indirect(l6[:]), COPY, scale=sb_t[:, 0:1])
                read_w[0] = [both_w[:, half(0)], both_w[:, half(1)]]
                read_v[0] = [both_v[:, half(0)], both_v[:, half(1)]]
            else:
                read_w[t][0] = early[:, 2 * t - 2, :]
                read_v[t][0] = early[:, 2 * t - 1, :]
                read_boards(t, 0)

        def second_product(h, planes_tag, banks):
            planes = sbuf([P, PACK, HALF], BF16, "planes%d" % h, planes_tag)
            for t in range(PACK - 1):
                nc.vector.tensor_tensor(planes[:, t, :], read_w[t][h], read_v[t][h], MAX)
            quarters = (slice(0, HALF // 2), slice(HALF // 2, HALF))
            for cols in quarters:
                nc.vector.tensor_tensor(planes[:, PACK - 1, cols], read_w[PACK - 1][h][:, cols], read_v[PACK - 1][h][:, cols], MAX)
            woven = sbuf([P, HALF, PACK], BF16, "woven%d" % h)
            for cols in quarters:
                nc.vector.tensor_copy(
                    woven[:, cols, :].rearrange("p (c i) t -> p c t i", i=4),
                    planes[:, :, cols].rearrange("p t (c i) -> p c t i", i=4),
                )
            codes = sbuf([P, HALF], U32, "codes%d" % h)
            scales = sbuf([P, HALF], U8, "scales%d" % h)
            for cols in quarters:
                nc.vector.quantize_mx(codes[:, cols].bitcast(FP8X4), scales[:, cols], woven[:, cols, :].rearrange("p o t -> p (o t)"))
            results = []
            for nt in range(2):
                acc = psum.tile([P, HALF], F32, name="p_%d_%d" % (h, nt), tag=banks[nt])
                nc.tensor.matmul_mx(
                    out=acc[:],
                    lhsT=wb_w[:, 2 * P * nt : 2 * P * (nt + 1)].bitcast(FP4X4),
                    lhsT_scale=wb_s[:, P * nt : P * (nt + 1)],
                    rhs=codes[:].bitcast(FP8X4),
                    rhs_scale=scales[:],
                    start=True,
                    stop=True,
                )
                result = sbuf([P, HALF], F32, "result_%d_%d" % (h, nt))
                nc.vector.tensor_copy(result[:], acc[:])
                results.append(result)
            return results

        first = second_product(0, "planes0", ("bank5", "bank6"))

        late = sbuf([P, 2 * (PACK - 1), HALF], F32, "late", "change3")
        for t in range(1, PACK):
            read_w[t][1] = late[:, 2 * t - 2, :]
            read_v[t][1] = late[:, 2 * t - 1, :]
            read_boards(t, 1)
        for nt in range(2):
            nc.scalar.activation(page[nt][:].indirect(list_half(l7, 0)), first[nt][:], COPY)

        second = second_product(1, "woven0", ("bank7", "bank0"))
        for nt in range(2):
            nc.scalar.activation(page[nt][:].indirect(list_half(l7, 1)), second[nt][:], COPY)
            for piece in range(U // STORE_COLS):
                lo, hi = piece * STORE_COLS, (piece + 1) * STORE_COLS
                steps = sbuf([P, STORE_COLS], F32, "steps_%d_%d" % (nt, piece))
                if piece == 0:
                    if nt == 0:
                        nc.vector.tensor_copy(steps[:, 0:1], page[nt][:, 0:1])
                    else:
                        nc.scalar.copy(steps[:, 0:1], page[nt][:, 0:1])
                    nc.vector.tensor_tensor(steps[:, 1:], page[nt][:, 1:hi], page[nt][:, 0 : hi - 1], SUB)
                else:
                    nc.vector.tensor_tensor(steps[:], page[nt][:, lo:hi], page[nt][:, lo - 1 : hi - 1], SUB)
                nc.sync.dma_start(out[nt * P : (nt + 1) * P, lo:hi], steps[:])
